import numpy as np
import ml_dtypes


def mxq(x, axis, fmt="e4m3"):
    dtype, down = {"e4m3": (ml_dtypes.float8_e4m3fn, 7), "e5m2": (ml_dtypes.float8_e5m2, 14)}[fmt]
    v = np.moveaxis(np.asarray(x, np.float32).astype(ml_dtypes.bfloat16).astype(np.float64), axis, -1)
    blocks = v.reshape(v.shape[:-1] + (-1, 32))
    amax = np.abs(blocks).max(-1, keepdims=True)
    byte = np.maximum(np.where(amax > 0, np.frexp(amax)[1] - 1 + 127, 0) - down, 1)
    scale = np.exp2(byte - 127.0)
    codes = (blocks / scale).astype(np.float32).astype(dtype).astype(np.float64)
    return np.moveaxis((codes * scale).reshape(v.shape), -1, axis)


WIDE = False


def mx_kscale(k):
    if not WIDE:
        return np.ones(k)
    levels = np.array([10, -10, 5, -5, 0])
    if k % 512:
        return np.exp2(np.random.permutation(np.resize(levels, k // 32))).repeat(32)
    a = np.empty((k // 512, 16))
    for p in range(k // 512):
        a[p, :8] = np.random.permutation(np.resize(levels, 8))
        for g in range(8):
            far = levels[np.abs(levels - a[p, g]) >= 10]
            a[p, g + 8] = far[np.random.randint(len(far))]
    return np.exp2(a.ravel()).repeat(32)


BF16 = ml_dtypes.bfloat16


def bf(x):
    return np.asarray(x, np.float32).astype(BF16)


def f64(x):
    return np.asarray(x).astype(np.float64)


E2M1 = np.array([0.0, 0.5, 1.0, 1.5, 2.0, 3.0, 4.0, 6.0, -0.0, -0.5, -1.0, -1.5, -2.0, -3.0, -4.0, -6.0])


def pack_weight(w, fmt):
    k, n = w.shape
    w = f64(bf(w)).reshape(k // 32, 32, n)
    amax = np.abs(w).max(1)
    if fmt == "e4m3":
        byte = np.frexp(amax)[1] - 1 + 127 - 7
    else:
        mant, ex = np.frexp(amax / 6.0)
        byte = np.where(mant > 0.5, ex, ex - 1) + 127
    byte = np.clip(np.where(amax > 0, byte, 1), 1, 254)
    scaled = (w * np.exp2(127.0 - byte)[:, None, :]).reshape(k, n).astype(np.float32)
    by_word = np.ascontiguousarray(scaled.reshape(k // 512, 128, 4, n).transpose(0, 1, 3, 2))
    if fmt == "e4m3":
        words = by_word.astype(ml_dtypes.float8_e4m3fn).view(np.uint8)
    else:
        c = by_word.astype(ml_dtypes.float4_e2m1fn).view(np.uint8) & 0xF
        words = c[..., 0::2] | (c[..., 1::2] << 4)
    return np.ascontiguousarray(words), np.ascontiguousarray(byte.astype(np.uint8).reshape(k // 512, 16, n))


def unpack_weight(words, scales, fmt):
    g, p, n, _ = words.shape
    if fmt == "e4m3":
        vals = np.ascontiguousarray(words).view(ml_dtypes.float8_e4m3fn).astype(np.float64)
    else:
        nib = np.empty((g, p, n, 4), np.uint8)
        nib[..., 0::2] = words & 0xF
        nib[..., 1::2] = words >> 4
        vals = E2M1[nib]
    vals = vals * np.repeat(np.exp2(scales.astype(np.float64) - 127.0), 8, axis=1)[..., None]
    return vals.transpose(0, 1, 3, 2).reshape(g * 512, n)
def pack4(w):
    words, scales = pack_weight(w, "e2m1")
    return words.reshape(words.shape[0], 128, -1), scales


def unpack4(words, scales):
    return unpack_weight(words.reshape(words.shape[0], 128, -1, 2), scales, "e2m1")


M, K, N, R, S = 1024, 2048, 1024, 1536, 512


def draw0():
    s, t, u = mx_kscale(K), mx_kscale(N), mx_kscale(M)
    ut = u[:, None] * t
    rgb_words, rgb_scales = pack4(np.random.standard_normal((N, R)) / np.sqrt(N) / t[:, None])
    return {"h": bf(np.random.standard_normal((M, K)) * s),
            "w": bf(np.random.standard_normal((K, N)) / np.sqrt(K) / s[:, None] * t),
            "x": bf(np.random.standard_normal((M, N)) * ut),
            "ratio": bf(np.random.uniform(0.4, 1.4, M) * u),
            "lim": bf(np.random.uniform(1.2, 1.8, (M, N)) * ut),
            "rgb_words": rgb_words,
            "rgb_scales": rgb_scales,
            "down": bf(np.random.standard_normal((S, M)) / np.sqrt(M) / u)}


def core(h, w, x, ratio, lim, rgb_words, rgb_scales, down):
    eps = mxq(f64(h), 1, "e4m3") @ mxq(f64(w), 0, "e4m3")
    bound = f64(lim)
    x0 = np.clip(f64(x) - f64(ratio)[:, None] * eps, -bound, bound)
    rgb = mxq(x0, 1, "e4m3") @ unpack4(rgb_words, rgb_scales)
    coarse = mxq(f64(down), 1, "e4m3") @ mxq(x0, 0, "e4m3")
    return rgb, coarse


def e4m3fn_bytes(y):
    return np.clip(np.asarray(y, np.float64), -448.0, 448.0).astype(np.float32).astype(ml_dtypes.float8_e4m3fn).view(np.uint8)


def e4m3fn_values(b):
    return np.asarray(b, np.uint8).view(ml_dtypes.float8_e4m3fn).astype(np.float64)


def setup_inputs():
    d = draw0()
    x0 = np.asarray(d['h']).astype(np.float64)
    s = (np.max(np.abs(x0), axis=(0,), keepdims=True) / 448.0).astype(np.float32)
    out = {}
    for k, v in d.items():
        if k == 'h':
            out['h_bytes'] = e4m3fn_bytes(x0 / s.astype(np.float64))
            out['h_scale'] = s
        else:
            out[k] = v
    return out


def reference(h_bytes, h_scale, w, x, ratio, lim, rgb_words, rgb_scales, down):
    return core(e4m3fn_values(h_bytes) * h_scale.astype(np.float64), w, x, ratio, lim, rgb_words, rgb_scales, down)

@@ -1,0 +1,429 @@
+from contextlib import ExitStack
+
+import concourse.mybir as mybir
+from concourse.masks import make_identity
+
+F32 = mybir.dt.float32
+BF16 = mybir.dt.bfloat16
+I32 = mybir.dt.int32
+U32 = mybir.dt.uint32
+U8 = mybir.dt.uint8
+FP8 = mybir.dt.float8_e4m3fn
+FP8X4 = mybir.dt.float8_e4m3fn_x4
+FP4X4 = mybir.dt.float4_e2m1fn_x4
+MULT = mybir.AluOpType.mult
+ADD = mybir.AluOpType.add
+MIN = mybir.AluOpType.min
+MAX = mybir.AluOpType.max
+
+M, K, N, R, S = 1024, 2048, 1024, 1536, 512
+FLOPS = 2 * (M * K * N + M * N * R + S * M * N)
+
+P = 128
+PACK = 4
+KP = P * PACK
+NT = 512
+HP = K // KP
+GM = M // KP
+MT = M // P
+HALVES = N // NT
+ST = S // P
+RT = R // NT
+
+LEAD = 3
+W_ON_VECTOR = ((0, 0), (2, 0), (0, 1))
+PATCH_ON_VECTOR = ((1, 1),)
+RGB_ON_VECTOR = ()
+
+
+def tile_ddim_clean_latent_rgb_s8_kernel(
+    tc, h_bytes, h_scale, w, x, ratio, lim, rgb_words, rgb_scales, down, rgb_out, coarse_out
+):
+    nc = tc.nc
+
+    h_rows = h_bytes.rearrange("(G p t) k -> G t p k", p=P, t=PACK)
+    w_rows = w.rearrange("(g p t) n -> g p t n", p=P, t=PACK)
+    x_rows = x.rearrange("(G p t) n -> G p t n", p=P, t=PACK)
+    lim_rows = lim.rearrange("(G p t) n -> G p t n", p=P, t=PACK)
+    down_rows = down.rearrange("(j p) m -> j p m", p=P)
+    rgb_rows = rgb_out.rearrange("(G p t) r -> G t p r", p=P, t=PACK)
+    coarse_rows = coarse_out.rearrange("(j p) n -> j p n", p=P)
+
+    with ExitStack() as ctx:
+        keep = ctx.enter_context(tc.tile_pool(name="keep", bufs=1))
+        ring = ctx.enter_context(tc.tile_pool(name="ring", bufs=2))
+        psum = ctx.enter_context(tc.psum_pool(name="psum", bufs=2))
+
+        scale_cols = keep.tile([P, 16], F32, name="scale_cols")
+        nc.sync.dma_start(out=scale_cols[:], in_=h_scale.rearrange("o (q c) -> (o q) c", c=16))
+        ratio_bf = keep.tile([P, GM, PACK], BF16, name="ratio_bf")
+        nc.scalar.dma_start(out=ratio_bf[:], in_=ratio.rearrange("(G p t) -> p G t", p=P, t=PACK))
+
+        h_raw = {}
+        w_raw = {}
+        x_in = {}
+        lim_in = {}
+
+        def load_h(i):
+            t = ring.tile([P, K], U8, name="h_raw", tag="h_raw", bufs=8, align_bytes=64)
+            nc.sync.dma_start(out=t[:], in_=h_rows[i // PACK, i % PACK])
+            h_raw[i] = t
+
+        def load_w(g, hf):
+            t = ring.tile([P, PACK, NT], BF16, name="w_raw", tag="w_raw", bufs=6, align_bytes=64)
+            nc.sync.dma_start(out=t[:], in_=w_rows[g][:, :, hf * NT : (hf + 1) * NT])
+            w_raw[g, hf] = t
+
+        def load_x(gm, hf):
+            t = ring.tile([P, PACK, NT], BF16, name="x_in", tag="x_in", bufs=4, align_bytes=64)
+            nc.sync.dma_start(out=t[:], in_=x_rows[gm][:, :, hf * NT : (hf + 1) * NT])
+            x_in[gm, hf] = t
+            l = ring.tile([P, PACK, NT], BF16, name="lim_in", tag="lim_in", bufs=4, align_bytes=64)
+            nc.sync.dma_start(out=l[:], in_=lim_rows[gm][:, :, hf * NT : (hf + 1) * NT])
+            lim_in[gm, hf] = l
+
+        ident = keep.tile([P, P], F32, name="ident", align_bytes=64)
+        make_identity(nc, ident[:])
+        c_scales = keep.tile([P, GM * R], U8, name="c_scales", align_bytes=64)
+        nc.gpsimd.memset(c_scales[:].bitcast(I32), 0)
+        c_words = keep.tile([P, GM, 2 * R], U8, name="c_words", align_bytes=64)
+
+        def load_c():
+            nc.sync.dma_start(out=c_words[:], in_=rgb_words.rearrange("g p b -> p g b"))
+            planes = rgb_scales.bitcast(I32).rearrange("g (q r) n -> r q g n", r=4)
+            for r in range(4):
+                nc.sync.dma_start(
+                    out=c_scales[:].bitcast(I32)[r:P:32, :].rearrange("q (g n) -> q g n", g=GM), in_=planes[r]
+                )
+
+        load_h(0)
+        load_w(0, 0)
+        load_w(1, 0)
+        load_h(1)
+        load_w(2, 0)
+        load_w(3, 0)
+        load_x(0, 0)
+        load_w(0, 1)
+        load_w(1, 1)
+
+        neg_ratio = keep.tile([P, MT], F32, name="neg_ratio")
+        nc.vector.tensor_scalar(
+            out=neg_ratio[:], in0=ratio_bf[:].rearrange("p G t -> p (G t)"), scalar1=-1.0, scalar2=None, op0=MULT
+        )
+
+        scale_all = keep.tile([P, K], F32, name="scale_all", align_bytes=64)
+        for b in range(4):
+            bank = psum.tile([P, 4, P], F32, name="tp", tag="tp", bufs=3)
+            for c in range(4):
+                col = 4 * b + c
+                nc.tensor.transpose(bank[:, c, :], scale_cols[:, col : col + 1].to_broadcast([P, P]), ident[:])
+            dst = scale_all[:].rearrange("p (q b c) -> p b q c", b=4, c=4)[:, b]
+            src = bank[:].rearrange("p c q -> p q c")
+            if b % 2 == 0:
+                nc.vector.tensor_copy(out=dst, in_=src)
+            else:
+                nc.scalar.copy(out=dst, in_=src)
+
+        w_codes = {}
+        w_planes = {}
+        w_grouped = {}
+
+        def w_interleave(g, hf):
+            t = ring.tile([P, NT * PACK], BF16, name="w_grouped", tag="w_grouped", bufs=2, align_bytes=64)
+            dst = t[:].rearrange("p (c i t) -> p c t i", i=4, t=PACK)
+            src = w_raw[g, hf][:].rearrange("p t (c i) -> p c t i", i=4)
+            if (g, hf) in W_ON_VECTOR:
+                nc.vector.tensor_copy(out=dst, in_=src)
+            else:
+                nc.scalar.copy(out=dst, in_=src)
+            w_grouped[g, hf] = t
+
+        def w_quant(g, hf):
+            c = keep.tile([P, NT], U32, name=f"w_codes{g}{hf}", align_bytes=64)
+            s = keep.tile([P, NT], U8, name=f"w_planes{g}{hf}", align_bytes=64)
+            nc.vector.quantize_mx(out=c[:].bitcast(FP8X4), scales=s[:], in_=w_grouped[g, hf][:])
+            w_codes[g, hf] = c
+            w_planes[g, hf] = s
+
+        h_scaled = {}
+        h_grouped = {}
+        h_codes = {}
+        h_planes = {}
+
+        def h_scale_rows(i):
+            for a in range(2):
+                t = ring.tile([P, K // 2], BF16, name="h_scaled", tag="h_scaled", bufs=4, align_bytes=64)
+                cols = slice(a * K // 2, (a + 1) * K // 2)
+                nc.vector.tensor_tensor(
+                    out=t[:], in0=h_raw[i][:, cols].bitcast(FP8), in1=scale_all[:, cols], op=MULT
+                )
+                h_scaled[i, a] = t
+
+        def h_turn(i):
+            grouped = ring.tile([P, HP * P * PACK], BF16, name="h_grouped", tag="h_grouped", bufs=2, align_bytes=64)
+            out_words = grouped[:].bitcast(F32).rearrange("p (a g r u) -> p a g r u", a=2, g=2, u=2)
+            for a in range(2):
+                words = h_scaled[i, a][:].bitcast(F32)
+                bank = psum.tile([P, 2, 2, P], F32, name="tp", tag="tp", bufs=3)
+                for g in range(2):
+                    for u in range(2):
+                        nc.tensor.transpose(bank[:, g, u, :], words[:, 256 * g + u : 256 * (g + 1) : 2], ident[:])
+                nc.scalar.copy(out=out_words[:, a], in_=bank[:].rearrange("p g u r -> p g r u"))
+            h_grouped[i] = grouped
+
+        def h_quant(i):
+            c = ring.tile([P, HP * P], U32, name="h_codes", tag="h_codes", bufs=4, align_bytes=64)
+            s = ring.tile([P, HP * P], U8, name="h_planes", tag="h_planes", bufs=4, align_bytes=64)
+            nc.vector.quantize_mx(out=c[:].bitcast(FP8X4), scales=s[:], in_=h_grouped[i][:])
+            h_codes[i] = c
+            h_planes[i] = s
+
+        eps = {}
+
+        def eps_mm(i, hf):
+            acc = psum.tile([P, NT], F32, name="ep", tag="ep", bufs=2)
+            for g in range(HP):
+                cols = slice(g * P, (g + 1) * P)
+                nc.tensor.matmul_mx(
+                    out=acc[:],
+                    lhsT=h_codes[i][:, cols].bitcast(FP8X4),
+                    lhsT_scale=h_planes[i][:, cols],
+                    rhs=w_codes[g, hf][:].bitcast(FP8X4),
+                    rhs_scale=w_planes[g, hf][:],
+                    start=(g == 0),
+                    stop=(g == HP - 1),
+                )
+            eps[i, hf] = acc
+
+        neg_lim = {}
+
+        def negate_lim(gm, hf):
+            t = ring.tile([P, PACK, NT], BF16, name="neg_lim", tag="neg_lim", bufs=2, align_bytes=64)
+            nc.vector.tensor_scalar(out=t[:], in0=lim_in[gm, hf][:], scalar1=-1.0, scalar2=None, op0=MULT)
+            neg_lim[gm, hf] = t
+
+        x0 = {}
+        for gm in range(GM):
+            x0[gm] = keep.tile([P, PACK, N], BF16, name=f"x0_{gm}", align_bytes=64)
+
+        def clean(i, hf):
+            gm, t = i // PACK, i % PACK
+            v = ring.tile([P, NT], BF16, name="v", tag="v", bufs=3, align_bytes=64)
+            nc.vector.scalar_tensor_tensor(
+                out=v[:], in0=eps[i, hf][:], scalar=neg_ratio[:, i : i + 1], in1=x_in[gm, hf][:, t, :], op0=MULT, op1=ADD
+            )
+            y = ring.tile([P, NT], BF16, name="y", tag="y", bufs=3, align_bytes=64)
+            nc.vector.tensor_tensor(out=y[:], in0=v[:], in1=lim_in[gm, hf][:, t, :], op=MIN)
+            nc.vector.tensor_tensor(
+                out=x0[gm][:, t, hf * NT : (hf + 1) * NT], in0=y[:], in1=neg_lim[gm, hf][:, t, :], op=MAX
+            )
+
+        xc_grouped = {}
+        xc_codes = {}
+        xc_planes = {}
+
+        def x0_turn(i):
+            gm, t = i // PACK, i % PACK
+            bank = psum.tile([P, 2, 2, P], F32, name="tp", tag="tp", bufs=3)
+            words = x0[gm][:, t, :].bitcast(F32)
+            for g in range(2):
+                for u in range(2):
+                    nc.tensor.transpose(bank[:, g, u, :], words[:, 256 * g + u : 256 * (g + 1) : 2], ident[:])
+            grouped = ring.tile([P, N], BF16, name="xc_grouped", tag="xc_grouped", bufs=2, align_bytes=64)
+            nc.scalar.copy(
+                out=grouped[:].bitcast(F32).rearrange("p (g r u) -> p g r u", g=2, u=2),
+                in_=bank[:].rearrange("p g u r -> p g r u"),
+            )
+            xc_grouped[i] = grouped
+
+        def x0_quant(i):
+            c = ring.tile([P, 2 * P], U32, name="xc_codes", tag="xc_codes", bufs=3, align_bytes=64)
+            s = ring.tile([P, 2 * P], U8, name="xc_planes", tag="xc_planes", bufs=3, align_bytes=64)
+            nc.vector.quantize_mx(out=c[:].bitcast(FP8X4), scales=s[:], in_=xc_grouped[i][:])
+            xc_codes[i] = c
+            xc_planes[i] = s
+
+        def rgb(i):
+            for b in range(RT):
+                stage = ring.tile([P, NT], F32, name="out_sb", tag="out_sb", bufs=6, align_bytes=64)
+                acc = psum.tile([P, NT], F32, name="mm", tag="mm", bufs=3)
+                for g in range(2):
+                    cols = slice(g * P, (g + 1) * P)
+                    nc.tensor.matmul_mx(
+                        out=acc[:],
+                        lhsT=xc_codes[i][:, cols].bitcast(FP8X4),
+                        lhsT_scale=xc_planes[i][:, cols],
+                        rhs=c_words[:, g, 2 * NT * b : 2 * NT * (b + 1)].bitcast(FP4X4),
+                        rhs_scale=c_scales[:, R * g + NT * b : R * g + NT * (b + 1)],
+                        start=(g == 0),
+                        stop=(g == 1),
+                    )
+                if (i, b) in RGB_ON_VECTOR:
+                    nc.vector.tensor_copy(out=stage[:], in_=acc[:])
+                else:
+                    nc.scalar.copy(out=stage[:], in_=acc[:])
+                nc.sync.dma_start(out=rgb_rows[i // PACK, i % PACK][:, b * NT : (b + 1) * NT], in_=stage[:])
+
+        xp_grouped = {}
+        xp_codes = {}
+        xp_planes = {}
+
+        def patch_interleave(gm, hf):
+            t = ring.tile([P, NT * PACK], BF16, name="xp_grouped", tag="xp_grouped", bufs=2, align_bytes=64)
+            dst = t[:].rearrange("p (c i t) -> p c t i", i=4, t=PACK)
+            src = x0[gm][:, :, hf * NT : (hf + 1) * NT].rearrange("p t (c i) -> p c t i", i=4)
+            if (gm, hf) in PATCH_ON_VECTOR:
+                nc.vector.tensor_copy(out=dst, in_=src)
+            else:
+                nc.scalar.copy(out=dst, in_=src)
+            xp_grouped[gm, hf] = t
+
+        def patch_quant(gm, hf):
+            c = keep.tile([P, NT], U32, name=f"xp_codes{gm}{hf}", align_bytes=64)
+            s = keep.tile([P, NT], U8, name=f"xp_planes{gm}{hf}", align_bytes=64)
+            nc.vector.quantize_mx(out=c[:].bitcast(FP8X4), scales=s[:], in_=xp_grouped[gm, hf][:])
+            xp_codes[gm, hf] = c
+            xp_planes[gm, hf] = s
+
+        d_raw = {}
+        d_grouped = {}
+        d_codes = {}
+        d_planes = {}
+
+        def load_down(j):
+            t = ring.tile([P, M], BF16, name="d_raw", tag="d_raw", bufs=2, align_bytes=64)
+            nc.sync.dma_start(out=t[:], in_=down_rows[j])
+            d_raw[j] = t
+
+        def down_turn(j):
+            bank = psum.tile([P, 2, 2, P], F32, name="tp", tag="tp", bufs=3)
+            words = d_raw[j][:].bitcast(F32)
+            for g in range(2):
+                for u in range(2):
+                    nc.tensor.transpose(bank[:, g, u, :], words[:, 256 * g + u : 256 * (g + 1) : 2], ident[:])
+            grouped = ring.tile([P, M], BF16, name="d_grouped", tag="d_grouped", bufs=2, align_bytes=64)
+            nc.scalar.copy(
+                out=grouped[:].bitcast(F32).rearrange("p (g r u) -> p g r u", g=2, u=2),
+                in_=bank[:].rearrange("p g u r -> p g r u"),
+            )
+            d_grouped[j] = grouped
+
+        def down_quant(j):
+            c = keep.tile([P, 2 * P], U32, name=f"d_codes{j}", align_bytes=64)
+            s = keep.tile([P, 2 * P], U8, name=f"d_planes{j}", align_bytes=64)
+            nc.vector.quantize_mx(out=c[:].bitcast(FP8X4), scales=s[:], in_=d_grouped[j][:])
+            d_codes[j] = c
+            d_planes[j] = s
+
+        def coarse(hf):
+            for j in range(ST):
+                acc = psum.tile([P, NT], F32, name="mm", tag="mm", bufs=3)
+                for gm in range(GM):
+                    cols = slice(gm * P, (gm + 1) * P)
+                    nc.tensor.matmul_mx(
+                        out=acc[:],
+                        lhsT=d_codes[j][:, cols].bitcast(FP8X4),
+                        lhsT_scale=d_planes[j][:, cols],
+                        rhs=xp_codes[gm, hf][:].bitcast(FP8X4),
+                        rhs_scale=xp_planes[gm, hf][:],
+                        start=(gm == 0),
+                        stop=(gm == GM - 1),
+                    )
+                stage = ring.tile([P, NT], F32, name="out_sb", tag="out_sb", bufs=6, align_bytes=64)
+                if j % 2 == 0:
+                    nc.vector.tensor_copy(out=stage[:], in_=acc[:])
+                else:
+                    nc.scalar.copy(out=stage[:], in_=acc[:])
+                nc.sync.dma_start(out=coarse_rows[j][:, hf * NT : (hf + 1) * NT], in_=stage[:])
+
+        h_scale_rows(0)
+        w_interleave(0, 0)
+        w_interleave(1, 0)
+        w_quant(0, 0)
+        h_turn(0)
+        w_interleave(2, 0)
+        w_quant(1, 0)
+        h_quant(0)
+        w_interleave(3, 0)
+        w_quant(2, 0)
+        h_scale_rows(1)
+        w_quant(3, 0)
+        eps_mm(0, 0)
+        h_turn(1)
+        load_w(2, 1)
+        load_w(3, 1)
+        load_x(0, 1)
+        for i in range(2, 4):
+            load_h(i)
+        load_c()
+        load_h(4)
+        load_x(1, 0)
+        load_h(5)
+        load_x(1, 1)
+        load_h(6)
+        load_h(7)
+        load_down(0)
+        load_down(1)
+        w_interleave(0, 1)
+        w_interleave(1, 1)
+        negate_lim(0, 0)
+        w_quant(0, 1)
+        w_quant(1, 1)
+        h_quant(1)
+        clean(0, 0)
+        eps_mm(1, 0)
+        w_interleave(2, 1)
+        w_interleave(3, 1)
+        w_quant(2, 1)
+        h_scale_rows(2)
+        w_quant(3, 1)
+        eps_mm(0, 1)
+        h_turn(2)
+        clean(1, 0)
+        negate_lim(0, 1)
+        clean(0, 1)
+        eps_mm(1, 1)
+        h_quant(2)
+        h_scale_rows(3)
+        x0_turn(0)
+        h_turn(3)
+        clean(1, 1)
+        eps_mm(2, 0)
+        eps_mm(2, 1)
+        x0_quant(0)
+        rgb(0)
+        for i in range(2, MT + 2):
+            gm = i // PACK
+            if i + 2 < MT:
+                h_scale_rows(i + 2)
+            if i < MT:
+                if i == PACK:
+                    negate_lim(1, 0)
+                    negate_lim(1, 1)
+                clean(i, 0)
+                clean(i, 1)
+            if i + 1 < MT:
+                h_quant(i + 1)
+            if i - 1 < MT:
+                x0_turn(i - 1)
+            if i + 2 < MT:
+                h_turn(i + 2)
+            if i + 1 < MT:
+                eps_mm(i + 1, 0)
+                eps_mm(i + 1, 1)
+            if i - 1 < MT:
+                x0_quant(i - 1)
+                rgb(i - 1)
+            if i % PACK == PACK - 1:
+                patch_interleave(gm, 0)
+                patch_interleave(gm, 1)
+                patch_quant(gm, 0)
+                patch_quant(gm, 1)
+            if i in (4, 5):
+                for j in (2 * (i - 4), 2 * (i - 4) + 1):
+                    down_turn(j)
+                    down_quant(j)
+                    if j + 2 < ST:
+                        load_down(j + 2)
+        coarse(0)
+        coarse(1)

@@ -30,10 +30,8 @@ HALVES = N // NT
 ST = S // P
 RT = R // NT
 
-LEAD = 3
-W_ON_VECTOR = ((0, 0), (2, 0), (0, 1))
-PATCH_ON_VECTOR = ((1, 1),)
-RGB_ON_VECTOR = ()
+SCALE_ON_VECTOR = (0, 2)
+W_ON_VECTOR = ((0, 0), (2, 0), (3, 1))
 
 
 def tile_ddim_clean_latent_rgb_s8_kernel(
@@ -54,34 +52,34 @@ def tile_ddim_clean_latent_rgb_s8_kernel(
         ring = ctx.enter_context(tc.tile_pool(name="ring", bufs=2))
         psum = ctx.enter_context(tc.psum_pool(name="psum", bufs=2))
 
-        scale_cols = keep.tile([P, 16], F32, name="scale_cols")
-        nc.sync.dma_start(out=scale_cols[:], in_=h_scale.rearrange("o (q c) -> (o q) c", c=16))
-        ratio_bf = keep.tile([P, GM, PACK], BF16, name="ratio_bf")
-        nc.scalar.dma_start(out=ratio_bf[:], in_=ratio.rearrange("(G p t) -> p G t", p=P, t=PACK))
-
-        h_raw = {}
-        w_raw = {}
-        x_in = {}
-        lim_in = {}
+        h_raw, w_raw, x_in, lim_in, d_raw = {}, {}, {}, {}, {}
 
         def load_h(i):
             t = ring.tile([P, K], U8, name="h_raw", tag="h_raw", bufs=8, align_bytes=64)
             nc.sync.dma_start(out=t[:], in_=h_rows[i // PACK, i % PACK])
             h_raw[i] = t
 
-        def load_w(g, hf):
-            t = ring.tile([P, PACK, NT], BF16, name="w_raw", tag="w_raw", bufs=6, align_bytes=64)
-            nc.sync.dma_start(out=t[:], in_=w_rows[g][:, :, hf * NT : (hf + 1) * NT])
-            w_raw[g, hf] = t
+        def load_wide(name, rows):
+            t = ring.tile([P, PACK, N], BF16, name=name, tag="wide", bufs=6, align_bytes=64)
+            nc.sync.dma_start(out=t[:], in_=rows)
+            return t
 
-        def load_x(gm, hf):
-            t = ring.tile([P, PACK, NT], BF16, name="x_in", tag="x_in", bufs=4, align_bytes=64)
-            nc.sync.dma_start(out=t[:], in_=x_rows[gm][:, :, hf * NT : (hf + 1) * NT])
-            x_in[gm, hf] = t
-            l = ring.tile([P, PACK, NT], BF16, name="lim_in", tag="lim_in", bufs=4, align_bytes=64)
-            nc.sync.dma_start(out=l[:], in_=lim_rows[gm][:, :, hf * NT : (hf + 1) * NT])
-            lim_in[gm, hf] = l
+        def load_w(g):
+            w_raw[g] = load_wide("w_raw", w_rows[g])
 
+        def load_x(gm):
+            x_in[gm] = load_wide("x_in", x_rows[gm])
+            lim_in[gm] = load_wide("lim_in", lim_rows[gm])
+
+        def load_down(j):
+            t = ring.tile([P, M], BF16, name="d_raw", tag="d_raw", bufs=4, align_bytes=64)
+            nc.sync.dma_start(out=t[:], in_=down_rows[j])
+            d_raw[j] = t
+
+        scale_cols = keep.tile([P, 16], F32, name="scale_cols")
+        nc.sync.dma_start(out=scale_cols[:], in_=h_scale.rearrange("o (q c) -> (o q) c", c=16))
+        ratio_bf = keep.tile([P, GM, PACK], BF16, name="ratio_bf")
+        nc.scalar.dma_start(out=ratio_bf[:], in_=ratio.rearrange("(G p t) -> p G t", p=P, t=PACK))
         ident = keep.tile([P, P], F32, name="ident", align_bytes=64)
         make_identity(nc, ident[:])
         c_scales = keep.tile([P, GM * R], U8, name="c_scales", align_bytes=64)
@@ -96,21 +94,29 @@ def tile_ddim_clean_latent_rgb_s8_kernel(
                     out=c_scales[:].bitcast(I32)[r:P:32, :].rearrange("q (g n) -> q g n", g=GM), in_=planes[r]
                 )
 
+        load_w(0)
         load_h(0)
-        load_w(0, 0)
-        load_w(1, 0)
+        load_w(1)
+        load_w(2)
         load_h(1)
-        load_w(2, 0)
-        load_w(3, 0)
-        load_x(0, 0)
-        load_w(0, 1)
-        load_w(1, 1)
+        load_w(3)
+        load_down(0)
+        load_down(1)
+        load_x(0)
+        load_h(2)
+        load_down(2)
+        load_down(3)
+        load_h(3)
+        load_c()
+        load_h(4)
+        load_x(1)
+        for i in range(5, MT):
+            load_h(i)
 
         neg_ratio = keep.tile([P, MT], F32, name="neg_ratio")
         nc.vector.tensor_scalar(
             out=neg_ratio[:], in0=ratio_bf[:].rearrange("p G t -> p (G t)"), scalar1=-1.0, scalar2=None, op0=MULT
         )
-
         scale_all = keep.tile([P, K], F32, name="scale_all", align_bytes=64)
         for b in range(4):
             bank = psum.tile([P, 4, P], F32, name="tp", tag="tp", bufs=3)
@@ -119,64 +125,64 @@ def tile_ddim_clean_latent_rgb_s8_kernel(
                 nc.tensor.transpose(bank[:, c, :], scale_cols[:, col : col + 1].to_broadcast([P, P]), ident[:])
             dst = scale_all[:].rearrange("p (q b c) -> p b q c", b=4, c=4)[:, b]
             src = bank[:].rearrange("p c q -> p q c")
-            if b % 2 == 0:
+            if b in SCALE_ON_VECTOR:
                 nc.vector.tensor_copy(out=dst, in_=src)
             else:
                 nc.scalar.copy(out=dst, in_=src)
 
-        w_codes = {}
-        w_planes = {}
-        w_grouped = {}
-
-        def w_interleave(g, hf):
-            t = ring.tile([P, NT * PACK], BF16, name="w_grouped", tag="w_grouped", bufs=2, align_bytes=64)
-            dst = t[:].rearrange("p (c i t) -> p c t i", i=4, t=PACK)
-            src = w_raw[g, hf][:].rearrange("p t (c i) -> p c t i", i=4)
-            if (g, hf) in W_ON_VECTOR:
+        def interleave(engine_is_vector, out, in_):
+            dst = out.rearrange("p (c i t) -> p c t i", i=4, t=PACK)
+            src = in_.rearrange("p t (c i) -> p c t i", i=4)
+            if engine_is_vector:
                 nc.vector.tensor_copy(out=dst, in_=src)
             else:
                 nc.scalar.copy(out=dst, in_=src)
+
+        w_grouped, w_codes, w_planes = {}, {}, {}
+
+        def w_il(g, hf):
+            t = ring.tile([P, NT * PACK], BF16, name="w_grouped", tag="w_grouped", bufs=3, align_bytes=64)
+            interleave((g, hf) in W_ON_VECTOR, t[:], w_raw[g][:, :, hf * NT : (hf + 1) * NT])
             w_grouped[g, hf] = t
 
-        def w_quant(g, hf):
+        def w_q(g, hf):
             c = keep.tile([P, NT], U32, name=f"w_codes{g}{hf}", align_bytes=64)
             s = keep.tile([P, NT], U8, name=f"w_planes{g}{hf}", align_bytes=64)
             nc.vector.quantize_mx(out=c[:].bitcast(FP8X4), scales=s[:], in_=w_grouped[g, hf][:])
-            w_codes[g, hf] = c
-            w_planes[g, hf] = s
+            w_codes[g, hf], w_planes[g, hf] = c, s
 
-        h_scaled = {}
-        h_grouped = {}
-        h_codes = {}
-        h_planes = {}
+        h_scaled, h_bank, h_grouped, h_codes, h_planes = {}, {}, {}, {}, {}
 
-        def h_scale_rows(i):
-            for a in range(2):
-                t = ring.tile([P, K // 2], BF16, name="h_scaled", tag="h_scaled", bufs=4, align_bytes=64)
-                cols = slice(a * K // 2, (a + 1) * K // 2)
-                nc.vector.tensor_tensor(
-                    out=t[:], in0=h_raw[i][:, cols].bitcast(FP8), in1=scale_all[:, cols], op=MULT
+        def h_mul(i, parts=(0, 1)):
+            if i not in h_scaled:
+                h_scaled[i] = ring.tile([P, K], BF16, name="h_scaled", tag="h_scaled", bufs=2, align_bytes=64)
+            cols = slice(parts[0] * K // 2, (parts[-1] + 1) * K // 2)
+            nc.vector.tensor_tensor(
+                out=h_scaled[i][:, cols], in0=h_raw[i][:, cols].bitcast(FP8), in1=scale_all[:, cols], op=MULT
+            )
+
+        def h_tr(i, a):
+            words = h_scaled[i][:].bitcast(F32)
+            bank = psum.tile([P, 2, 2, P], F32, name="tp", tag="tp", bufs=3)
+            for g in range(2):
+                for u in range(2):
+                    first_word = 256 * (2 * a + g)
+                    nc.tensor.transpose(bank[:, g, u, :], words[:, first_word + u : first_word + 256 : 2], ident[:])
+            h_bank[i, a] = bank
+
+        def h_out(i, a):
+            if a == 0:
+                h_grouped[i] = ring.tile(
+                    [P, HP * P * PACK], BF16, name="h_grouped", tag="h_grouped", bufs=2, align_bytes=64
                 )
-                h_scaled[i, a] = t
+            out_words = h_grouped[i][:].bitcast(F32).rearrange("p (a g r u) -> p a g r u", a=2, g=2, u=2)
+            nc.scalar.copy(out=out_words[:, a], in_=h_bank[i, a][:].rearrange("p g u r -> p g r u"))
 
-        def h_turn(i):
-            grouped = ring.tile([P, HP * P * PACK], BF16, name="h_grouped", tag="h_grouped", bufs=2, align_bytes=64)
-            out_words = grouped[:].bitcast(F32).rearrange("p (a g r u) -> p a g r u", a=2, g=2, u=2)
-            for a in range(2):
-                words = h_scaled[i, a][:].bitcast(F32)
-                bank = psum.tile([P, 2, 2, P], F32, name="tp", tag="tp", bufs=3)
-                for g in range(2):
-                    for u in range(2):
-                        nc.tensor.transpose(bank[:, g, u, :], words[:, 256 * g + u : 256 * (g + 1) : 2], ident[:])
-                nc.scalar.copy(out=out_words[:, a], in_=bank[:].rearrange("p g u r -> p g r u"))
-            h_grouped[i] = grouped
-
-        def h_quant(i):
+        def h_q(i):
             c = ring.tile([P, HP * P], U32, name="h_codes", tag="h_codes", bufs=4, align_bytes=64)
             s = ring.tile([P, HP * P], U8, name="h_planes", tag="h_planes", bufs=4, align_bytes=64)
             nc.vector.quantize_mx(out=c[:].bitcast(FP8X4), scales=s[:], in_=h_grouped[i][:])
-            h_codes[i] = c
-            h_planes[i] = s
+            h_codes[i], h_planes[i] = c, s
 
         eps = {}
 
@@ -195,235 +201,304 @@ def tile_ddim_clean_latent_rgb_s8_kernel(
                 )
             eps[i, hf] = acc
 
-        neg_lim = {}
-
-        def negate_lim(gm, hf):
-            t = ring.tile([P, PACK, NT], BF16, name="neg_lim", tag="neg_lim", bufs=2, align_bytes=64)
-            nc.vector.tensor_scalar(out=t[:], in0=lim_in[gm, hf][:], scalar1=-1.0, scalar2=None, op0=MULT)
-            neg_lim[gm, hf] = t
-
-        x0 = {}
+        neg_lim, v_all, y_all, x0 = {}, {}, {}, {}
         for gm in range(GM):
             x0[gm] = keep.tile([P, PACK, N], BF16, name=f"x0_{gm}", align_bytes=64)
 
-        def clean(i, hf):
-            gm, t = i // PACK, i % PACK
-            v = ring.tile([P, NT], BF16, name="v", tag="v", bufs=3, align_bytes=64)
+        def lim_neg(i):
+            neg_lim[i] = ring.tile([P, N], BF16, name="neg_lim", tag="neg_lim", bufs=4, align_bytes=64)
+            nc.scalar.activation(
+                out=neg_lim[i][:], in_=lim_in[i // PACK][:, i % PACK, :], func=mybir.ActivationFunctionType.Copy, scale=-1.0
+            )
+
+        def v_of(i):
+            if i not in v_all:
+                v_all[i] = ring.tile([P, N], BF16, name="v", tag="v", bufs=3, align_bytes=64)
+                y_all[i] = ring.tile([P, N], BF16, name="y", tag="y", bufs=3, align_bytes=64)
+            return v_all[i], y_all[i]
+
+        def x_stt(i, hf):
+            v, y = v_of(i)
+            cols = slice(hf * NT, (hf + 1) * NT)
             nc.vector.scalar_tensor_tensor(
-                out=v[:], in0=eps[i, hf][:], scalar=neg_ratio[:, i : i + 1], in1=x_in[gm, hf][:, t, :], op0=MULT, op1=ADD
-            )
-            y = ring.tile([P, NT], BF16, name="y", tag="y", bufs=3, align_bytes=64)
-            nc.vector.tensor_tensor(out=y[:], in0=v[:], in1=lim_in[gm, hf][:, t, :], op=MIN)
-            nc.vector.tensor_tensor(
-                out=x0[gm][:, t, hf * NT : (hf + 1) * NT], in0=y[:], in1=neg_lim[gm, hf][:, t, :], op=MAX
+                out=v[:, cols],
+                in0=eps[i, hf][:],
+                scalar=neg_ratio[:, i : i + 1],
+                in1=x_in[i // PACK][:, i % PACK, cols],
+                op0=MULT,
+                op1=ADD,
             )
 
-        xc_grouped = {}
-        xc_codes = {}
-        xc_planes = {}
+        def x_min(i):
+            v, y = v_of(i)
+            nc.vector.tensor_tensor(out=y[:], in0=v[:], in1=lim_in[i // PACK][:, i % PACK, :], op=MIN)
 
-        def x0_turn(i):
+        def x_max(i):
+            v, y = v_of(i)
             gm, t = i // PACK, i % PACK
+            nc.vector.tensor_tensor(
+                out=x0[gm][:, t, :].rearrange("p (u q e) -> p q u e", u=2, e=2),
+                in0=y[:].rearrange("p (q u e) -> p q u e", u=2, e=2),
+                in1=neg_lim[i][:].rearrange("p (q u e) -> p q u e", u=2, e=2),
+                op=MAX,
+            )
+
+        xc_bank, xc_grouped, xc_codes, xc_planes = {}, {}, {}, {}
+
+        def xc_tr(i):
             bank = psum.tile([P, 2, 2, P], F32, name="tp", tag="tp", bufs=3)
-            words = x0[gm][:, t, :].bitcast(F32)
+            words = x0[i // PACK][:, i % PACK, :].bitcast(F32)
             for g in range(2):
                 for u in range(2):
-                    nc.tensor.transpose(bank[:, g, u, :], words[:, 256 * g + u : 256 * (g + 1) : 2], ident[:])
+                    first_word = 2 * P * u + P * g
+                    nc.tensor.transpose(bank[:, g, u, :], words[:, first_word : first_word + P], ident[:])
+            xc_bank[i] = bank
+
+        def xc_out(i):
             grouped = ring.tile([P, N], BF16, name="xc_grouped", tag="xc_grouped", bufs=2, align_bytes=64)
             nc.scalar.copy(
                 out=grouped[:].bitcast(F32).rearrange("p (g r u) -> p g r u", g=2, u=2),
-                in_=bank[:].rearrange("p g u r -> p g r u"),
+                in_=xc_bank[i][:].rearrange("p g u r -> p g r u"),
             )
             xc_grouped[i] = grouped
 
-        def x0_quant(i):
+        def xc_q(i):
             c = ring.tile([P, 2 * P], U32, name="xc_codes", tag="xc_codes", bufs=3, align_bytes=64)
             s = ring.tile([P, 2 * P], U8, name="xc_planes", tag="xc_planes", bufs=3, align_bytes=64)
             nc.vector.quantize_mx(out=c[:].bitcast(FP8X4), scales=s[:], in_=xc_grouped[i][:])
-            xc_codes[i] = c
-            xc_planes[i] = s
+            xc_codes[i], xc_planes[i] = c, s
 
-        def rgb(i):
-            for b in range(RT):
-                stage = ring.tile([P, NT], F32, name="out_sb", tag="out_sb", bufs=6, align_bytes=64)
-                acc = psum.tile([P, NT], F32, name="mm", tag="mm", bufs=3)
-                for g in range(2):
-                    cols = slice(g * P, (g + 1) * P)
-                    nc.tensor.matmul_mx(
-                        out=acc[:],
-                        lhsT=xc_codes[i][:, cols].bitcast(FP8X4),
-                        lhsT_scale=xc_planes[i][:, cols],
-                        rhs=c_words[:, g, 2 * NT * b : 2 * NT * (b + 1)].bitcast(FP4X4),
-                        rhs_scale=c_scales[:, R * g + NT * b : R * g + NT * (b + 1)],
-                        start=(g == 0),
-                        stop=(g == 1),
-                    )
-                if (i, b) in RGB_ON_VECTOR:
-                    nc.vector.tensor_copy(out=stage[:], in_=acc[:])
-                else:
-                    nc.scalar.copy(out=stage[:], in_=acc[:])
-                nc.sync.dma_start(out=rgb_rows[i // PACK, i % PACK][:, b * NT : (b + 1) * NT], in_=stage[:])
+        rgb_bank = {}
 
-        xp_grouped = {}
-        xp_codes = {}
-        xp_planes = {}
+        def rgb_mm(i, b):
+            acc = psum.tile([P, NT], F32, name="mm", tag="mm", bufs=3)
+            for g in range(2):
+                cols = slice(g * P, (g + 1) * P)
+                nc.tensor.matmul_mx(
+                    out=acc[:],
+                    lhsT=xc_codes[i][:, cols].bitcast(FP8X4),
+                    lhsT_scale=xc_planes[i][:, cols],
+                    rhs=c_words[:, g, 2 * NT * b : 2 * NT * (b + 1)].bitcast(FP4X4),
+                    rhs_scale=c_scales[:, R * g + NT * b : R * g + NT * (b + 1)],
+                    start=(g == 0),
+                    stop=(g == 1),
+                )
+            rgb_bank[i, b] = acc
 
-        def patch_interleave(gm, hf):
-            t = ring.tile([P, NT * PACK], BF16, name="xp_grouped", tag="xp_grouped", bufs=2, align_bytes=64)
-            dst = t[:].rearrange("p (c i t) -> p c t i", i=4, t=PACK)
-            src = x0[gm][:, :, hf * NT : (hf + 1) * NT].rearrange("p t (c i) -> p c t i", i=4)
-            if (gm, hf) in PATCH_ON_VECTOR:
-                nc.vector.tensor_copy(out=dst, in_=src)
+        def rgb_out(i, b, vector=False):
+            stage = ring.tile([P, NT], F32, name="out_sb", tag="out_sb", bufs=10, align_bytes=64)
+            if vector:
+                nc.vector.tensor_copy(out=stage[:], in_=rgb_bank[i, b][:])
             else:
-                nc.scalar.copy(out=dst, in_=src)
-            xp_grouped[gm, hf] = t
+                nc.scalar.copy(out=stage[:], in_=rgb_bank[i, b][:])
+            nc.sync.dma_start(out=rgb_rows[i // PACK, i % PACK][:, b * NT : (b + 1) * NT], in_=stage[:])
 
-        def patch_quant(gm, hf):
+        xp_grouped, xp_codes, xp_planes = {}, {}, {}
+
+        def xp_il(gm, hf, u, vector=False):
+            if (gm, hf) not in xp_grouped:
+                xp_grouped[gm, hf] = ring.tile(
+                    [P, NT * PACK], BF16, name="xp_grouped", tag="w_grouped", bufs=3, align_bytes=64
+                )
+            n = NT // 2
+            lo = u * NT + hf * n
+            interleave(
+                vector, xp_grouped[gm, hf][:, u * n * PACK : (u + 1) * n * PACK], x0[gm][:, :, lo : lo + n]
+            )
+
+        def xp_q(gm, hf):
             c = keep.tile([P, NT], U32, name=f"xp_codes{gm}{hf}", align_bytes=64)
             s = keep.tile([P, NT], U8, name=f"xp_planes{gm}{hf}", align_bytes=64)
             nc.vector.quantize_mx(out=c[:].bitcast(FP8X4), scales=s[:], in_=xp_grouped[gm, hf][:])
-            xp_codes[gm, hf] = c
-            xp_planes[gm, hf] = s
+            xp_codes[gm, hf], xp_planes[gm, hf] = c, s
 
-        d_raw = {}
-        d_grouped = {}
-        d_codes = {}
-        d_planes = {}
+        d_bank, d_grouped, d_codes, d_planes = {}, {}, {}, {}
 
-        def load_down(j):
-            t = ring.tile([P, M], BF16, name="d_raw", tag="d_raw", bufs=2, align_bytes=64)
-            nc.sync.dma_start(out=t[:], in_=down_rows[j])
-            d_raw[j] = t
-
-        def down_turn(j):
+        def d_tr(j):
             bank = psum.tile([P, 2, 2, P], F32, name="tp", tag="tp", bufs=3)
             words = d_raw[j][:].bitcast(F32)
             for g in range(2):
                 for u in range(2):
                     nc.tensor.transpose(bank[:, g, u, :], words[:, 256 * g + u : 256 * (g + 1) : 2], ident[:])
-            grouped = ring.tile([P, M], BF16, name="d_grouped", tag="d_grouped", bufs=2, align_bytes=64)
+            d_bank[j] = bank
+
+        def d_out(j):
+            grouped = ring.tile([P, M], BF16, name="d_grouped", tag="d_grouped", bufs=4, align_bytes=64)
             nc.scalar.copy(
                 out=grouped[:].bitcast(F32).rearrange("p (g r u) -> p g r u", g=2, u=2),
-                in_=bank[:].rearrange("p g u r -> p g r u"),
+                in_=d_bank[j][:].rearrange("p g u r -> p g r u"),
             )
             d_grouped[j] = grouped
 
-        def down_quant(j):
+        def d_q(j):
             c = keep.tile([P, 2 * P], U32, name=f"d_codes{j}", align_bytes=64)
             s = keep.tile([P, 2 * P], U8, name=f"d_planes{j}", align_bytes=64)
             nc.vector.quantize_mx(out=c[:].bitcast(FP8X4), scales=s[:], in_=d_grouped[j][:])
-            d_codes[j] = c
-            d_planes[j] = s
+            d_codes[j], d_planes[j] = c, s
 
-        def coarse(hf):
-            for j in range(ST):
+        coarse_bank = {}
+
+        def coarse_mm(hf, j):
+            if j < 2:
+                acc = psum.tile([P, NT], F32, name="ep", tag="ep", bufs=2)
+            else:
                 acc = psum.tile([P, NT], F32, name="mm", tag="mm", bufs=3)
-                for gm in range(GM):
-                    cols = slice(gm * P, (gm + 1) * P)
-                    nc.tensor.matmul_mx(
-                        out=acc[:],
-                        lhsT=d_codes[j][:, cols].bitcast(FP8X4),
-                        lhsT_scale=d_planes[j][:, cols],
-                        rhs=xp_codes[gm, hf][:].bitcast(FP8X4),
-                        rhs_scale=xp_planes[gm, hf][:],
-                        start=(gm == 0),
-                        stop=(gm == GM - 1),
-                    )
-                stage = ring.tile([P, NT], F32, name="out_sb", tag="out_sb", bufs=6, align_bytes=64)
-                if j % 2 == 0:
-                    nc.vector.tensor_copy(out=stage[:], in_=acc[:])
-                else:
-                    nc.scalar.copy(out=stage[:], in_=acc[:])
-                nc.sync.dma_start(out=coarse_rows[j][:, hf * NT : (hf + 1) * NT], in_=stage[:])
+            for gm in range(GM):
+                cols = slice(gm * P, (gm + 1) * P)
+                nc.tensor.matmul_mx(
+                    out=acc[:],
+                    lhsT=d_codes[j][:, cols].bitcast(FP8X4),
+                    lhsT_scale=d_planes[j][:, cols],
+                    rhs=xp_codes[gm, hf][:].bitcast(FP8X4),
+                    rhs_scale=xp_planes[gm, hf][:],
+                    start=(gm == 0),
+                    stop=(gm == GM - 1),
+                )
+            coarse_bank[hf, j] = acc
 
-        h_scale_rows(0)
-        w_interleave(0, 0)
-        w_interleave(1, 0)
-        w_quant(0, 0)
-        h_turn(0)
-        w_interleave(2, 0)
-        w_quant(1, 0)
-        h_quant(0)
-        w_interleave(3, 0)
-        w_quant(2, 0)
-        h_scale_rows(1)
-        w_quant(3, 0)
+        def coarse_put(hf, j, vector):
+            stage = ring.tile([P, NT], F32, name="out_sb", tag="out_sb", bufs=10, align_bytes=64)
+            dst = stage[:].rearrange("p (q u e) -> p q u e", u=2, e=2)
+            src = coarse_bank[hf, j][:].rearrange("p (u q e) -> p q u e", u=2, e=2)
+            if vector:
+                nc.vector.tensor_copy(out=dst, in_=src)
+            else:
+                nc.scalar.copy(out=dst, in_=src)
+            nc.sync.dma_start(out=coarse_rows[j][:, hf * NT : (hf + 1) * NT], in_=stage[:])
+
+        ctx.enter_context(tc.manual_schedule())
+        w_il(0, 0)
+        w_il(0, 1)
+        h_mul(0, (0,))
+        h_mul(0, (1,))
+        h_tr(0, 0)
+        h_tr(0, 1)
+        h_out(0, 0)
+        h_out(0, 1)
+        w_q(0, 0)
+        w_q(0, 1)
+        w_il(1, 0)
+        h_q(0)
+        w_il(2, 0)
+        w_q(2, 0)
+        w_q(1, 0)
+        h_mul(1, (0,))
+        w_il(3, 0)
+        h_mul(1, (1,))
+        w_q(3, 0)
         eps_mm(0, 0)
-        h_turn(1)
-        load_w(2, 1)
-        load_w(3, 1)
-        load_x(0, 1)
-        for i in range(2, 4):
-            load_h(i)
-        load_c()
-        load_h(4)
-        load_x(1, 0)
-        load_h(5)
-        load_x(1, 1)
-        load_h(6)
-        load_h(7)
-        load_down(0)
-        load_down(1)
-        w_interleave(0, 1)
-        w_interleave(1, 1)
-        negate_lim(0, 0)
-        w_quant(0, 1)
-        w_quant(1, 1)
-        h_quant(1)
-        clean(0, 0)
-        eps_mm(1, 0)
-        w_interleave(2, 1)
-        w_interleave(3, 1)
-        w_quant(2, 1)
-        h_scale_rows(2)
-        w_quant(3, 1)
+        w_il(1, 1)
+        w_il(3, 1)
+        h_tr(1, 0)
+        h_tr(1, 1)
+        d_tr(0)
+        h_out(1, 0)
+        h_out(1, 1)
+        w_q(3, 1)
+        w_q(1, 1)
+        w_il(2, 1)
+        h_q(1)
+        h_mul(2, (0,))
+        x_stt(0, 0)
+        d_out(0)
+        lim_neg(0)
+        w_q(2, 1)
+        d_tr(1)
         eps_mm(0, 1)
-        h_turn(2)
-        clean(1, 0)
-        negate_lim(0, 1)
-        clean(0, 1)
-        eps_mm(1, 1)
-        h_quant(2)
-        h_scale_rows(3)
-        x0_turn(0)
-        h_turn(3)
-        clean(1, 1)
-        eps_mm(2, 0)
-        eps_mm(2, 1)
-        x0_quant(0)
-        rgb(0)
-        for i in range(2, MT + 2):
-            gm = i // PACK
+        eps_mm(1, 0)
+        d_out(1)
+        h_mul(2, (1,))
+        for i in range(MT - 2):
+            if i >= 1:
+                xc_tr(i - 1)
+                xc_out(i - 1)
             if i + 2 < MT:
-                h_scale_rows(i + 2)
-            if i < MT:
-                if i == PACK:
-                    negate_lim(1, 0)
-                    negate_lim(1, 1)
-                clean(i, 0)
-                clean(i, 1)
-            if i + 1 < MT:
-                h_quant(i + 1)
-            if i - 1 < MT:
-                x0_turn(i - 1)
-            if i + 2 < MT:
-                h_turn(i + 2)
-            if i + 1 < MT:
+                h_tr(i + 2, 0)
+                h_tr(i + 2, 1)
+                h_out(i + 2, 0)
+                h_out(i + 2, 1)
+            if i == 0:
+                d_tr(2)
+                d_tr(3)
+            lim_neg(i + 1)
+            if i == 0:
+                d_out(2)
+                d_out(3)
+            if i >= 2:
+                for b in range(RT):
+                    rgb_out(i - 2, b)
+            if i >= 1:
+                x_stt(i, 0)
+            x_stt(i, 1)
+            if i >= 1:
                 eps_mm(i + 1, 0)
-                eps_mm(i + 1, 1)
-            if i - 1 < MT:
-                x0_quant(i - 1)
-                rgb(i - 1)
-            if i % PACK == PACK - 1:
-                patch_interleave(gm, 0)
-                patch_interleave(gm, 1)
-                patch_quant(gm, 0)
-                patch_quant(gm, 1)
+            eps_mm(i + 1, 1)
             if i in (4, 5):
-                for j in (2 * (i - 4), 2 * (i - 4) + 1):
-                    down_turn(j)
-                    down_quant(j)
-                    if j + 2 < ST:
-                        load_down(j + 2)
-        coarse(0)
-        coarse(1)
+                xp_il(0, 0, i - 4)
+            if i >= 1:
+                xc_q(i - 1)
+            x_min(i)
+            if i + 3 < MT:
+                h_mul(i + 3)
+            x_max(i)
+            if i + 2 < MT:
+                h_q(i + 2)
+            if 1 <= i < 3:
+                d_q(2 * i - 2)
+                d_q(2 * i - 1)
+            if i == 5:
+                xp_il(0, 1, 0, vector=True)
+            if i >= 1:
+                for b in range(RT):
+                    rgb_mm(i - 1, b)
+        i = MT - 2
+        xc_tr(i - 1)
+        xc_out(i - 1)
+        lim_neg(i + 1)
+        for b in range(RT):
+            rgb_out(i - 2, b)
+        x_stt(i, 0)
+        x_stt(i, 1)
+        eps_mm(i + 1, 0)
+        eps_mm(i + 1, 1)
+        x_min(i)
+        xc_q(i - 1)
+        x_max(i)
+        xc_tr(i)
+        xc_out(i)
+        for b in range(RT):
+            rgb_mm(i - 1, b)
+        xp_il(0, 1, 1, vector=True)
+        xp_q(0, 0)
+        xp_q(0, 1)
+        for b in range(RT):
+            rgb_out(i - 1, b)
+        x_stt(i + 1, 0)
+        x_stt(i + 1, 1)
+        xc_q(i)
+        x_min(i + 1)
+        x_max(i + 1)
+        for b in range(RT):
+            rgb_mm(i, b)
+        xc_tr(i + 1)
+        rgb_out(i, 0)
+        xc_out(i + 1)
+        rgb_out(i, 1)
+        rgb_out(i, 2)
+        i = MT - 1
+        xp_il(1, 0, 0, vector=True)
+        xp_il(1, 0, 1, vector=True)
+        xc_q(i)
+        xp_q(1, 0)
+        for b in range(RT):
+            rgb_mm(i, b)
+            rgb_out(i, b)
+        xp_il(1, 1, 0, vector=True)
+        xp_il(1, 1, 1, vector=True)
+        xp_q(1, 1)
+        for j in range(ST):
+            coarse_mm(0, j)
+            coarse_put(0, j, vector=(j % 2 == 1))
+        for j in range(ST):
+            coarse_mm(1, j)
+            coarse_put(1, j, vector=(j % 2 == 1))

@@ -100,12 +100,10 @@ def tile_ddim_clean_latent_rgb_s8_kernel(
         load_w(2)
         load_h(1)
         load_w(3)
-        load_down(0)
-        load_down(1)
-        load_x(0)
+        for j in range(ST):
+            load_down(j)
         load_h(2)
-        load_down(2)
-        load_down(3)
+        load_x(0)
         load_h(3)
         load_c()
         load_h(4)
@@ -184,22 +182,24 @@ def tile_ddim_clean_latent_rgb_s8_kernel(
             nc.vector.quantize_mx(out=c[:].bitcast(FP8X4), scales=s[:], in_=h_grouped[i][:])
             h_codes[i], h_planes[i] = c, s
 
-        eps = {}
+        eps, eps_done = {}, {}
 
-        def eps_mm(i, hf):
-            acc = psum.tile([P, NT], F32, name="ep", tag="ep", bufs=2)
-            for g in range(HP):
+        def eps_mm(i, hf, passes=tuple(range(HP)), tag="ep"):
+            if (i, hf) not in eps:
+                eps[i, hf] = psum.tile([P, NT], F32, name=tag, tag=tag, bufs={"ep": 2, "mm": 3}[tag])
+                eps_done[i, hf] = 0
+            for g in passes:
                 cols = slice(g * P, (g + 1) * P)
                 nc.tensor.matmul_mx(
-                    out=acc[:],
+                    out=eps[i, hf][:],
                     lhsT=h_codes[i][:, cols].bitcast(FP8X4),
                     lhsT_scale=h_planes[i][:, cols],
                     rhs=w_codes[g, hf][:].bitcast(FP8X4),
                     rhs_scale=w_planes[g, hf][:],
-                    start=(g == 0),
-                    stop=(g == HP - 1),
+                    start=(eps_done[i, hf] == 0),
+                    stop=(eps_done[i, hf] == HP - 1),
                 )
-            eps[i, hf] = acc
+                eps_done[i, hf] += 1
 
         neg_lim, v_all, y_all, x0 = {}, {}, {}, {}
         for gm in range(GM):
@@ -315,7 +315,10 @@ def tile_ddim_clean_latent_rgb_s8_kernel(
         d_bank, d_grouped, d_codes, d_planes = {}, {}, {}, {}
 
         def d_tr(j):
-            bank = psum.tile([P, 2, 2, P], F32, name="tp", tag="tp", bufs=3)
+            if j < 1:
+                bank = psum.tile([P, 2, 2, P], F32, name="mm", tag="mm", bufs=3)
+            else:
+                bank = psum.tile([P, 2, 2, P], F32, name="tp", tag="tp", bufs=3)
             words = d_raw[j][:].bitcast(F32)
             for g in range(2):
                 for u in range(2):
@@ -371,92 +374,94 @@ def tile_ddim_clean_latent_rgb_s8_kernel(
         w_il(0, 1)
         h_mul(0, (0,))
         h_mul(0, (1,))
-        h_tr(0, 0)
-        h_tr(0, 1)
-        h_out(0, 0)
-        h_out(0, 1)
         w_q(0, 0)
         w_q(0, 1)
+        h_tr(0, 0)
+        h_tr(0, 1)
         w_il(1, 0)
-        h_q(0)
+        h_out(0, 0)
+        h_out(0, 1)
         w_il(2, 0)
-        w_q(2, 0)
         w_q(1, 0)
+        w_q(2, 0)
         h_mul(1, (0,))
         w_il(3, 0)
+        h_q(0)
         h_mul(1, (1,))
         w_q(3, 0)
+        d_tr(0)
         eps_mm(0, 0)
         w_il(1, 1)
         w_il(3, 1)
         h_tr(1, 0)
         h_tr(1, 1)
-        d_tr(0)
+        d_tr(3)
         h_out(1, 0)
         h_out(1, 1)
         w_q(3, 1)
         w_q(1, 1)
+        eps_mm(0, 1, (0, 3, 1))
         w_il(2, 1)
         h_q(1)
+        eps_mm(1, 0, tag="mm")
+        eps_mm(1, 1, (0, 3, 1), tag="mm")
         h_mul(2, (0,))
         x_stt(0, 0)
         d_out(0)
         lim_neg(0)
         w_q(2, 1)
-        d_tr(1)
-        eps_mm(0, 1)
-        eps_mm(1, 0)
-        d_out(1)
+        eps_mm(0, 1, (2,))
+        eps_mm(1, 1, (2,))
+        d_out(3)
         h_mul(2, (1,))
         for i in range(MT - 2):
-            if i >= 1:
-                xc_tr(i - 1)
-                xc_out(i - 1)
             if i + 2 < MT:
                 h_tr(i + 2, 0)
                 h_tr(i + 2, 1)
                 h_out(i + 2, 0)
                 h_out(i + 2, 1)
             if i == 0:
+                d_tr(1)
                 d_tr(2)
-                d_tr(3)
+            if i >= 1:
+                xc_tr(i - 1)
+                xc_out(i - 1)
             lim_neg(i + 1)
             if i == 0:
+                d_out(1)
                 d_out(2)
-                d_out(3)
-            if i >= 2:
-                for b in range(RT):
-                    rgb_out(i - 2, b)
+            if i in (4, 5):
+                xp_il(0, 0, i - 4)
             if i >= 1:
                 x_stt(i, 0)
             x_stt(i, 1)
             if i >= 1:
                 eps_mm(i + 1, 0)
-            eps_mm(i + 1, 1)
-            if i in (4, 5):
-                xp_il(0, 0, i - 4)
+                eps_mm(i + 1, 1)
+            if i + 3 < MT:
+                h_mul(i + 3, (0,))
+            x_min(i)
+            if i == 5:
+                for j in range(ST):
+                    d_q(j)
             if i >= 1:
                 xc_q(i - 1)
-            x_min(i)
-            if i + 3 < MT:
-                h_mul(i + 3)
             x_max(i)
+            if i + 3 < MT:
+                h_mul(i + 3, (1,))
             if i + 2 < MT:
                 h_q(i + 2)
-            if 1 <= i < 3:
-                d_q(2 * i - 2)
-                d_q(2 * i - 1)
             if i == 5:
                 xp_il(0, 1, 0, vector=True)
+                xp_il(0, 1, 1, vector=True)
             if i >= 1:
                 for b in range(RT):
                     rgb_mm(i - 1, b)
+                    rgb_out(i - 1, b)
         i = MT - 2
         xc_tr(i - 1)
         xc_out(i - 1)
         lim_neg(i + 1)
-        for b in range(RT):
-            rgb_out(i - 2, b)
         x_stt(i, 0)
         x_stt(i, 1)
         eps_mm(i + 1, 0)
@@ -464,41 +469,42 @@ def tile_ddim_clean_latent_rgb_s8_kernel(
         x_min(i)
         xc_q(i - 1)
         x_max(i)
+        xp_q(0, 0)
         xc_tr(i)
         xc_out(i)
         for b in range(RT):
             rgb_mm(i - 1, b)
-        xp_il(0, 1, 1, vector=True)
-        xp_q(0, 0)
-        xp_q(0, 1)
-        for b in range(RT):
             rgb_out(i - 1, b)
         x_stt(i + 1, 0)
         x_stt(i + 1, 1)
         xc_q(i)
         x_min(i + 1)
+        xp_q(0, 1)
         x_max(i + 1)
         for b in range(RT):
             rgb_mm(i, b)
-        xc_tr(i + 1)
-        rgb_out(i, 0)
-        xc_out(i + 1)
-        rgb_out(i, 1)
-        rgb_out(i, 2)
         i = MT - 1
+        xc_tr(i)
         xp_il(1, 0, 0, vector=True)
         xp_il(1, 0, 1, vector=True)
-        xc_q(i)
         xp_q(1, 0)
-        for b in range(RT):
-            rgb_mm(i, b)
-            rgb_out(i, b)
-        xp_il(1, 1, 0, vector=True)
-        xp_il(1, 1, 1, vector=True)
-        xp_q(1, 1)
+        rgb_out(i - 1, 0)
+        rgb_out(i - 1, 1)
+        xc_out(i)
+        rgb_out(i - 1, 2)
         for j in range(ST):
             coarse_mm(0, j)
-            coarse_put(0, j, vector=(j % 2 == 1))
+        xp_il(1, 1, 0, vector=True)
+        xc_q(i)
+        xp_il(1, 1, 1, vector=True)
+        xp_q(1, 1)
+        coarse_put(0, 0, vector=False)
+        coarse_put(0, 1, vector=False)
+        coarse_put(0, 2, vector=False)
+        coarse_put(0, 3, vector=True)
+        for b in range(RT):
+            rgb_mm(i, b)
+            rgb_out(i, b, vector=(b == 1))
         for j in range(ST):
             coarse_mm(1, j)
-            coarse_put(1, j, vector=(j % 2 == 1))
+            coarse_put(1, j, vector=(j % 2 == 0))

@@ -30,7 +30,7 @@ HALVES = N // NT
 ST = S // P
 RT = R // NT
 
-SCALE_ON_VECTOR = (0, 2)
+SCALE_ON_VECTOR = (0, 1)
 W_ON_VECTOR = ((0, 0), (2, 0), (3, 1))
 
 
@@ -52,6 +52,7 @@ def tile_ddim_clean_latent_rgb_s8_kernel(
         ring = ctx.enter_context(tc.tile_pool(name="ring", bufs=2))
         psum = ctx.enter_context(tc.psum_pool(name="psum", bufs=2))
 
+        ctx.enter_context(tc.manual_schedule())
         h_raw, w_raw, x_in, lim_in, d_raw = {}, {}, {}, {}, {}
 
         def load_h(i):
@@ -100,10 +101,10 @@ def tile_ddim_clean_latent_rgb_s8_kernel(
         load_w(2)
         load_h(1)
         load_w(3)
-        for j in range(ST):
-            load_down(j)
         load_h(2)
         load_x(0)
+        for j in range(ST):
+            load_down(j)
         load_h(3)
         load_c()
         load_h(4)
@@ -112,8 +113,11 @@ def tile_ddim_clean_latent_rgb_s8_kernel(
             load_h(i)
 
         neg_ratio = keep.tile([P, MT], F32, name="neg_ratio")
-        nc.vector.tensor_scalar(
-            out=neg_ratio[:], in0=ratio_bf[:].rearrange("p G t -> p (G t)"), scalar1=-1.0, scalar2=None, op0=MULT
+        nc.scalar.activation(
+            out=neg_ratio[:],
+            in_=ratio_bf[:].rearrange("p G t -> p (G t)"),
+            func=mybir.ActivationFunctionType.Copy,
+            scale=-1.0,
         )
         scale_all = keep.tile([P, K], F32, name="scale_all", align_bytes=64)
         for b in range(4):
@@ -200,6 +204,11 @@ def tile_ddim_clean_latent_rgb_s8_kernel(
                     stop=(eps_done[i, hf] == HP - 1),
                 )
                 eps_done[i, hf] += 1
+
+        def keep_busy(count):
+            idle = psum.tile([P, NT], F32, name="ep", tag="ep", bufs=2)
+            for n in range(count):
+                nc.tensor.matmul(idle[:], h_scaled[2][:, 0:P], h_scaled[2][:, 0:NT], start=True, stop=True)
 
         neg_lim, v_all, y_all, x0 = {}, {}, {}, {}
         for gm in range(GM):
@@ -369,7 +378,6 @@ def tile_ddim_clean_latent_rgb_s8_kernel(
                 nc.scalar.copy(out=dst, in_=src)
             nc.sync.dma_start(out=coarse_rows[j][:, hf * NT : (hf + 1) * NT], in_=stage[:])
 
-        ctx.enter_context(tc.manual_schedule())
         w_il(0, 0)
         w_il(0, 1)
         h_mul(0, (0,))
@@ -389,13 +397,11 @@ def tile_ddim_clean_latent_rgb_s8_kernel(
         h_q(0)
         h_mul(1, (1,))
         w_q(3, 0)
-        d_tr(0)
         eps_mm(0, 0)
         w_il(1, 1)
         w_il(3, 1)
         h_tr(1, 0)
         h_tr(1, 1)
-        d_tr(3)
         h_out(1, 0)
         h_out(1, 1)
         w_q(3, 1)
@@ -407,12 +413,10 @@ def tile_ddim_clean_latent_rgb_s8_kernel(
         eps_mm(1, 1, (0, 3, 1), tag="mm")
         h_mul(2, (0,))
         x_stt(0, 0)
-        d_out(0)
         lim_neg(0)
         w_q(2, 1)
         eps_mm(0, 1, (2,))
         eps_mm(1, 1, (2,))
-        d_out(3)
         h_mul(2, (1,))
         for i in range(MT - 2):
             if i + 2 < MT:
@@ -421,15 +425,16 @@ def tile_ddim_clean_latent_rgb_s8_kernel(
                 h_out(i + 2, 0)
                 h_out(i + 2, 1)
             if i == 0:
-                d_tr(1)
-                d_tr(2)
+                for j in range(ST):
+                    d_tr(j)
+                keep_busy(3)
             if i >= 1:
                 xc_tr(i - 1)
                 xc_out(i - 1)
             lim_neg(i + 1)
             if i == 0:
-                d_out(1)
-                d_out(2)
+                for j in range(ST):
+                    d_out(j)
             if i in (4, 5):
                 xp_il(0, 0, i - 4)
             if i >= 1:
@@ -451,9 +456,6 @@ def tile_ddim_clean_latent_rgb_s8_kernel(
                 h_mul(i + 3, (1,))
             if i + 2 < MT:
                 h_q(i + 2)
-            if i == 5:
-                xp_il(0, 1, 0, vector=True)
-                xp_il(0, 1, 1, vector=True)
             if i >= 1:
                 for b in range(RT):
                     rgb_mm(i - 1, b)
@@ -467,9 +469,11 @@ def tile_ddim_clean_latent_rgb_s8_kernel(
         eps_mm(i + 1, 0)
         eps_mm(i + 1, 1)
         x_min(i)
-        xc_q(i - 1)
-        x_max(i)
         xp_q(0, 0)
+        x_max(i)
+        xp_il(0, 1, 0, vector=True)
+        xc_q(i - 1)
+        xp_il(0, 1, 1, vector=True)
         xc_tr(i)
         xc_out(i)
         for b in range(RT):
@@ -479,7 +483,6 @@ def tile_ddim_clean_latent_rgb_s8_kernel(
         x_stt(i + 1, 1)
         xc_q(i)
         x_min(i + 1)
-        xp_q(0, 1)
         x_max(i + 1)
         for b in range(RT):
             rgb_mm(i, b)
@@ -488,6 +491,7 @@ def tile_ddim_clean_latent_rgb_s8_kernel(
         xp_il(1, 0, 0, vector=True)
         xp_il(1, 0, 1, vector=True)
         xp_q(1, 0)
+        xp_q(0, 1)
         rgb_out(i - 1, 0)
         rgb_out(i - 1, 1)
         xc_out(i)

from contextlib import ExitStack

import concourse.mybir as mybir
from concourse.masks import make_identity

F32 = mybir.dt.float32
BF16 = mybir.dt.bfloat16
I32 = mybir.dt.int32
U32 = mybir.dt.uint32
U8 = mybir.dt.uint8
FP8 = mybir.dt.float8_e4m3fn
FP8X4 = mybir.dt.float8_e4m3fn_x4
FP4X4 = mybir.dt.float4_e2m1fn_x4
MULT = mybir.AluOpType.mult
ADD = mybir.AluOpType.add
MIN = mybir.AluOpType.min
MAX = mybir.AluOpType.max

M, K, N, R, S = 1024, 2048, 1024, 1536, 512
FLOPS = 2 * (M * K * N + M * N * R + S * M * N)

P = 128
PACK = 4
KP = P * PACK
NT = 512
HP = K // KP
GM = M // KP
MT = M // P
HALVES = N // NT
ST = S // P
RT = R // NT

SCALE_ON_VECTOR = (0, 1)
W_ON_VECTOR = ((0, 0), (2, 0), (3, 1))


def tile_ddim_clean_latent_rgb_s8_kernel(
    tc, h_bytes, h_scale, w, x, ratio, lim, rgb_words, rgb_scales, down, rgb_out, coarse_out
):
    nc = tc.nc

    h_rows = h_bytes.rearrange("(G p t) k -> G t p k", p=P, t=PACK)
    w_rows = w.rearrange("(g p t) n -> g p t n", p=P, t=PACK)
    x_rows = x.rearrange("(G p t) n -> G p t n", p=P, t=PACK)
    lim_rows = lim.rearrange("(G p t) n -> G p t n", p=P, t=PACK)
    down_rows = down.rearrange("(j p) m -> j p m", p=P)
    rgb_rows = rgb_out.rearrange("(G p t) r -> G t p r", p=P, t=PACK)
    coarse_rows = coarse_out.rearrange("(j p) n -> j p n", p=P)

    with ExitStack() as ctx:
        keep = ctx.enter_context(tc.tile_pool(name="keep", bufs=1))
        ring = ctx.enter_context(tc.tile_pool(name="ring", bufs=2))
        psum = ctx.enter_context(tc.psum_pool(name="psum", bufs=2))

        ctx.enter_context(tc.manual_schedule())
        h_raw, w_raw, x_in, lim_in, d_raw = {}, {}, {}, {}, {}

        def load_h(i):
            t = ring.tile([P, K], U8, name="h_raw", tag="h_raw", bufs=8, align_bytes=64)
            nc.sync.dma_start(out=t[:], in_=h_rows[i // PACK, i % PACK])
            h_raw[i] = t

        def load_wide(name, rows):
            t = ring.tile([P, PACK, N], BF16, name=name, tag="wide", bufs=6, align_bytes=64)
            nc.sync.dma_start(out=t[:], in_=rows)
            return t

        def load_w(g):
            w_raw[g] = load_wide("w_raw", w_rows[g])

        def load_x(gm):
            x_in[gm] = load_wide("x_in", x_rows[gm])
            lim_in[gm] = load_wide("lim_in", lim_rows[gm])

        def load_down(j):
            t = ring.tile([P, M], BF16, name="d_raw", tag="d_raw", bufs=4, align_bytes=64)
            nc.sync.dma_start(out=t[:], in_=down_rows[j])
            d_raw[j] = t

        scale_cols = keep.tile([P, 16], F32, name="scale_cols")
        nc.sync.dma_start(out=scale_cols[:], in_=h_scale.rearrange("o (q c) -> (o q) c", c=16))
        ratio_bf = keep.tile([P, GM, PACK], BF16, name="ratio_bf")
        nc.scalar.dma_start(out=ratio_bf[:], in_=ratio.rearrange("(G p t) -> p G t", p=P, t=PACK))
        ident = keep.tile([P, P], F32, name="ident", align_bytes=64)
        make_identity(nc, ident[:])
        c_scales = keep.tile([P, GM * R], U8, name="c_scales", align_bytes=64)
        nc.gpsimd.memset(c_scales[:].bitcast(I32), 0)
        c_words = keep.tile([P, GM, 2 * R], U8, name="c_words", align_bytes=64)

        def load_c():
            nc.sync.dma_start(out=c_words[:], in_=rgb_words.rearrange("g p b -> p g b"))
            planes = rgb_scales.bitcast(I32).rearrange("g (q r) n -> r q g n", r=4)
            for r in range(4):
                nc.sync.dma_start(
                    out=c_scales[:].bitcast(I32)[r:P:32, :].rearrange("q (g n) -> q g n", g=GM), in_=planes[r]
                )

        load_w(0)
        load_h(0)
        load_w(1)
        load_w(2)
        load_h(1)
        load_w(3)
        load_h(2)
        load_x(0)
        for j in range(ST):
            load_down(j)
        load_h(3)
        load_c()
        load_h(4)
        load_x(1)
        for i in range(5, MT):
            load_h(i)

        neg_ratio = keep.tile([P, MT], F32, name="neg_ratio")
        nc.scalar.activation(
            out=neg_ratio[:],
            in_=ratio_bf[:].rearrange("p G t -> p (G t)"),
            func=mybir.ActivationFunctionType.Copy,
            scale=-1.0,
        )
        scale_all = keep.tile([P, K], F32, name="scale_all", align_bytes=64)
        for b in range(4):
            bank = psum.tile([P, 4, P], F32, name="tp", tag="tp", bufs=3)
            for c in range(4):
                col = 4 * b + c
                nc.tensor.transpose(bank[:, c, :], scale_cols[:, col : col + 1].to_broadcast([P, P]), ident[:])
            dst = scale_all[:].rearrange("p (q b c) -> p b q c", b=4, c=4)[:, b]
            src = bank[:].rearrange("p c q -> p q c")
            if b in SCALE_ON_VECTOR:
                nc.vector.tensor_copy(out=dst, in_=src)
            else:
                nc.scalar.copy(out=dst, in_=src)

        def interleave(engine_is_vector, out, in_):
            dst = out.rearrange("p (c i t) -> p c t i", i=4, t=PACK)
            src = in_.rearrange("p t (c i) -> p c t i", i=4)
            if engine_is_vector:
                nc.vector.tensor_copy(out=dst, in_=src)
            else:
                nc.scalar.copy(out=dst, in_=src)

        w_grouped, w_codes, w_planes = {}, {}, {}

        def w_il(g, hf):
            t = ring.tile([P, NT * PACK], BF16, name="w_grouped", tag="w_grouped", bufs=3, align_bytes=64)
            interleave((g, hf) in W_ON_VECTOR, t[:], w_raw[g][:, :, hf * NT : (hf + 1) * NT])
            w_grouped[g, hf] = t

        def w_q(g, hf):
            c = keep.tile([P, NT], U32, name=f"w_codes{g}{hf}", align_bytes=64)
            s = keep.tile([P, NT], U8, name=f"w_planes{g}{hf}", align_bytes=64)
            nc.vector.quantize_mx(out=c[:].bitcast(FP8X4), scales=s[:], in_=w_grouped[g, hf][:])
            w_codes[g, hf], w_planes[g, hf] = c, s

        h_scaled, h_bank, h_grouped, h_codes, h_planes = {}, {}, {}, {}, {}

        def h_mul(i, parts=(0, 1)):
            if i not in h_scaled:
                h_scaled[i] = ring.tile([P, K], BF16, name="h_scaled", tag="h_scaled", bufs=2, align_bytes=64)
            cols = slice(parts[0] * K // 2, (parts[-1] + 1) * K // 2)
            nc.vector.tensor_tensor(
                out=h_scaled[i][:, cols], in0=h_raw[i][:, cols].bitcast(FP8), in1=scale_all[:, cols], op=MULT
            )

        def h_tr(i, a):
            words = h_scaled[i][:].bitcast(F32)
            bank = psum.tile([P, 2, 2, P], F32, name="tp", tag="tp", bufs=3)
            for g in range(2):
                for u in range(2):
                    first_word = 256 * (2 * a + g)
                    nc.tensor.transpose(bank[:, g, u, :], words[:, first_word + u : first_word + 256 : 2], ident[:])
            h_bank[i, a] = bank

        def h_out(i, a):
            if a == 0:
                h_grouped[i] = ring.tile(
                    [P, HP * P * PACK], BF16, name="h_grouped", tag="h_grouped", bufs=2, align_bytes=64
                )
            out_words = h_grouped[i][:].bitcast(F32).rearrange("p (a g r u) -> p a g r u", a=2, g=2, u=2)
            nc.scalar.copy(out=out_words[:, a], in_=h_bank[i, a][:].rearrange("p g u r -> p g r u"))

        def h_q(i):
            c = ring.tile([P, HP * P], U32, name="h_codes", tag="h_codes", bufs=4, align_bytes=64)
            s = ring.tile([P, HP * P], U8, name="h_planes", tag="h_planes", bufs=4, align_bytes=64)
            nc.vector.quantize_mx(out=c[:].bitcast(FP8X4), scales=s[:], in_=h_grouped[i][:])
            h_codes[i], h_planes[i] = c, s

        eps, eps_done = {}, {}

        def eps_mm(i, hf, passes=tuple(range(HP)), tag="ep"):
            if (i, hf) not in eps:
                eps[i, hf] = psum.tile([P, NT], F32, name=tag, tag=tag, bufs={"ep": 2, "mm": 3}[tag])
                eps_done[i, hf] = 0
            for g in passes:
                cols = slice(g * P, (g + 1) * P)
                nc.tensor.matmul_mx(
                    out=eps[i, hf][:],
                    lhsT=h_codes[i][:, cols].bitcast(FP8X4),
                    lhsT_scale=h_planes[i][:, cols],
                    rhs=w_codes[g, hf][:].bitcast(FP8X4),
                    rhs_scale=w_planes[g, hf][:],
                    start=(eps_done[i, hf] == 0),
                    stop=(eps_done[i, hf] == HP - 1),
                )
                eps_done[i, hf] += 1

        def keep_busy(count):
            idle = psum.tile([P, NT], F32, name="ep", tag="ep", bufs=2)
            for n in range(count):
                nc.tensor.matmul(idle[:], h_scaled[2][:, 0:P], h_scaled[2][:, 0:NT], start=True, stop=True)

        neg_lim, v_all, y_all, x0 = {}, {}, {}, {}
        for gm in range(GM):
            x0[gm] = keep.tile([P, PACK, N], BF16, name=f"x0_{gm}", align_bytes=64)

        def lim_neg(i):
            neg_lim[i] = ring.tile([P, N], BF16, name="neg_lim", tag="neg_lim", bufs=4, align_bytes=64)
            nc.scalar.activation(
                out=neg_lim[i][:], in_=lim_in[i // PACK][:, i % PACK, :], func=mybir.ActivationFunctionType.Copy, scale=-1.0
            )

        def v_of(i):
            if i not in v_all:
                v_all[i] = ring.tile([P, N], BF16, name="v", tag="v", bufs=3, align_bytes=64)
                y_all[i] = ring.tile([P, N], BF16, name="y", tag="y", bufs=3, align_bytes=64)
            return v_all[i], y_all[i]

        def x_stt(i, hf):
            v, y = v_of(i)
            cols = slice(hf * NT, (hf + 1) * NT)
            nc.vector.scalar_tensor_tensor(
                out=v[:, cols],
                in0=eps[i, hf][:],
                scalar=neg_ratio[:, i : i + 1],
                in1=x_in[i // PACK][:, i % PACK, cols],
                op0=MULT,
                op1=ADD,
            )

        def x_min(i):
            v, y = v_of(i)
            nc.vector.tensor_tensor(out=y[:], in0=v[:], in1=lim_in[i // PACK][:, i % PACK, :], op=MIN)

        def x_max(i):
            v, y = v_of(i)
            gm, t = i // PACK, i % PACK
            nc.vector.tensor_tensor(
                out=x0[gm][:, t, :].rearrange("p (u q e) -> p q u e", u=2, e=2),
                in0=y[:].rearrange("p (q u e) -> p q u e", u=2, e=2),
                in1=neg_lim[i][:].rearrange("p (q u e) -> p q u e", u=2, e=2),
                op=MAX,
            )

        xc_bank, xc_grouped, xc_codes, xc_planes = {}, {}, {}, {}

        def xc_tr(i):
            bank = psum.tile([P, 2, 2, P], F32, name="tp", tag="tp", bufs=3)
            words = x0[i // PACK][:, i % PACK, :].bitcast(F32)
            for g in range(2):
                for u in range(2):
                    first_word = 2 * P * u + P * g
                    nc.tensor.transpose(bank[:, g, u, :], words[:, first_word : first_word + P], ident[:])
            xc_bank[i] = bank

        def xc_out(i):
            grouped = ring.tile([P, N], BF16, name="xc_grouped", tag="xc_grouped", bufs=2, align_bytes=64)
            nc.scalar.copy(
                out=grouped[:].bitcast(F32).rearrange("p (g r u) -> p g r u", g=2, u=2),
                in_=xc_bank[i][:].rearrange("p g u r -> p g r u"),
            )
            xc_grouped[i] = grouped

        def xc_q(i):
            c = ring.tile([P, 2 * P], U32, name="xc_codes", tag="xc_codes", bufs=3, align_bytes=64)
            s = ring.tile([P, 2 * P], U8, name="xc_planes", tag="xc_planes", bufs=3, align_bytes=64)
            nc.vector.quantize_mx(out=c[:].bitcast(FP8X4), scales=s[:], in_=xc_grouped[i][:])
            xc_codes[i], xc_planes[i] = c, s

        rgb_bank = {}

        def rgb_mm(i, b):
            acc = psum.tile([P, NT], F32, name="mm", tag="mm", bufs=3)
            for g in range(2):
                cols = slice(g * P, (g + 1) * P)
                nc.tensor.matmul_mx(
                    out=acc[:],
                    lhsT=xc_codes[i][:, cols].bitcast(FP8X4),
                    lhsT_scale=xc_planes[i][:, cols],
                    rhs=c_words[:, g, 2 * NT * b : 2 * NT * (b + 1)].bitcast(FP4X4),
                    rhs_scale=c_scales[:, R * g + NT * b : R * g + NT * (b + 1)],
                    start=(g == 0),
                    stop=(g == 1),
                )
            rgb_bank[i, b] = acc

        def rgb_out(i, b, vector=False):
            stage = ring.tile([P, NT], F32, name="out_sb", tag="out_sb", bufs=10, align_bytes=64)
            if vector:
                nc.vector.tensor_copy(out=stage[:], in_=rgb_bank[i, b][:])
            else:
                nc.scalar.copy(out=stage[:], in_=rgb_bank[i, b][:])
            nc.sync.dma_start(out=rgb_rows[i // PACK, i % PACK][:, b * NT : (b + 1) * NT], in_=stage[:])

        xp_grouped, xp_codes, xp_planes = {}, {}, {}

        def xp_il(gm, hf, u, vector=False):
            if (gm, hf) not in xp_grouped:
                xp_grouped[gm, hf] = ring.tile(
                    [P, NT * PACK], BF16, name="xp_grouped", tag="w_grouped", bufs=3, align_bytes=64
                )
            n = NT // 2
            lo = u * NT + hf * n
            interleave(
                vector, xp_grouped[gm, hf][:, u * n * PACK : (u + 1) * n * PACK], x0[gm][:, :, lo : lo + n]
            )

        def xp_q(gm, hf):
            c = keep.tile([P, NT], U32, name=f"xp_codes{gm}{hf}", align_bytes=64)
            s = keep.tile([P, NT], U8, name=f"xp_planes{gm}{hf}", align_bytes=64)
            nc.vector.quantize_mx(out=c[:].bitcast(FP8X4), scales=s[:], in_=xp_grouped[gm, hf][:])
            xp_codes[gm, hf], xp_planes[gm, hf] = c, s

        d_bank, d_grouped, d_codes, d_planes = {}, {}, {}, {}

        def d_tr(j):
            if j < 1:
                bank = psum.tile([P, 2, 2, P], F32, name="mm", tag="mm", bufs=3)
            else:
                bank = psum.tile([P, 2, 2, P], F32, name="tp", tag="tp", bufs=3)
            words = d_raw[j][:].bitcast(F32)
            for g in range(2):
                for u in range(2):
                    nc.tensor.transpose(bank[:, g, u, :], words[:, 256 * g + u : 256 * (g + 1) : 2], ident[:])
            d_bank[j] = bank

        def d_out(j):
            grouped = ring.tile([P, M], BF16, name="d_grouped", tag="d_grouped", bufs=4, align_bytes=64)
            nc.scalar.copy(
                out=grouped[:].bitcast(F32).rearrange("p (g r u) -> p g r u", g=2, u=2),
                in_=d_bank[j][:].rearrange("p g u r -> p g r u"),
            )
            d_grouped[j] = grouped

        def d_q(j):
            c = keep.tile([P, 2 * P], U32, name=f"d_codes{j}", align_bytes=64)
            s = keep.tile([P, 2 * P], U8, name=f"d_planes{j}", align_bytes=64)
            nc.vector.quantize_mx(out=c[:].bitcast(FP8X4), scales=s[:], in_=d_grouped[j][:])
            d_codes[j], d_planes[j] = c, s

        coarse_bank = {}

        def coarse_mm(hf, j):
            if j < 2:
                acc = psum.tile([P, NT], F32, name="ep", tag="ep", bufs=2)
            else:
                acc = psum.tile([P, NT], F32, name="mm", tag="mm", bufs=3)
            for gm in range(GM):
                cols = slice(gm * P, (gm + 1) * P)
                nc.tensor.matmul_mx(
                    out=acc[:],
                    lhsT=d_codes[j][:, cols].bitcast(FP8X4),
                    lhsT_scale=d_planes[j][:, cols],
                    rhs=xp_codes[gm, hf][:].bitcast(FP8X4),
                    rhs_scale=xp_planes[gm, hf][:],
                    start=(gm == 0),
                    stop=(gm == GM - 1),
                )
            coarse_bank[hf, j] = acc

        def coarse_put(hf, j, vector):
            stage = ring.tile([P, NT], F32, name="out_sb", tag="out_sb", bufs=10, align_bytes=64)
            dst = stage[:].rearrange("p (q u e) -> p q u e", u=2, e=2)
            src = coarse_bank[hf, j][:].rearrange("p (u q e) -> p q u e", u=2, e=2)
            if vector:
                nc.vector.tensor_copy(out=dst, in_=src)
            else:
                nc.scalar.copy(out=dst, in_=src)
            nc.sync.dma_start(out=coarse_rows[j][:, hf * NT : (hf + 1) * NT], in_=stage[:])

        w_il(0, 0)
        w_il(0, 1)
        h_mul(0, (0,))
        h_mul(0, (1,))
        w_q(0, 0)
        w_q(0, 1)
        h_tr(0, 0)
        h_tr(0, 1)
        w_il(1, 0)
        h_out(0, 0)
        h_out(0, 1)
        w_il(2, 0)
        w_q(1, 0)
        w_q(2, 0)
        h_mul(1, (0,))
        w_il(3, 0)
        h_q(0)
        h_mul(1, (1,))
        w_q(3, 0)
        eps_mm(0, 0)
        w_il(1, 1)
        w_il(3, 1)
        h_tr(1, 0)
        h_tr(1, 1)
        h_out(1, 0)
        h_out(1, 1)
        w_q(3, 1)
        w_q(1, 1)
        eps_mm(0, 1, (0, 3, 1))
        w_il(2, 1)
        h_q(1)
        eps_mm(1, 0, tag="mm")
        eps_mm(1, 1, (0, 3, 1), tag="mm")
        h_mul(2, (0,))
        x_stt(0, 0)
        lim_neg(0)
        w_q(2, 1)
        eps_mm(0, 1, (2,))
        eps_mm(1, 1, (2,))
        h_mul(2, (1,))
        for i in range(MT - 2):
            if i + 2 < MT:
                h_tr(i + 2, 0)
                h_tr(i + 2, 1)
                h_out(i + 2, 0)
                h_out(i + 2, 1)
            if i == 0:
                for j in range(ST):
                    d_tr(j)
                keep_busy(3)
            if i >= 1:
                xc_tr(i - 1)
                xc_out(i - 1)
            lim_neg(i + 1)
            if i == 0:
                for j in range(ST):
                    d_out(j)
            if i in (4, 5):
                xp_il(0, 0, i - 4)
            if i >= 1:
                x_stt(i, 0)
            x_stt(i, 1)
            if i >= 1:
                eps_mm(i + 1, 0)
                eps_mm(i + 1, 1)
            if i + 3 < MT:
                h_mul(i + 3, (0,))
            x_min(i)
            if i == 5:
                for j in range(ST):
                    d_q(j)
            if i >= 1:
                xc_q(i - 1)
            x_max(i)
            if i + 3 < MT:
                h_mul(i + 3, (1,))
            if i + 2 < MT:
                h_q(i + 2)
            if i >= 1:
                for b in range(RT):
                    rgb_mm(i - 1, b)
                    rgb_out(i - 1, b)
        i = MT - 2
        xc_tr(i - 1)
        xc_out(i - 1)
        lim_neg(i + 1)
        x_stt(i, 0)
        x_stt(i, 1)
        eps_mm(i + 1, 0)
        eps_mm(i + 1, 1)
        x_min(i)
        xp_q(0, 0)
        x_max(i)
        xp_il(0, 1, 0, vector=True)
        xc_q(i - 1)
        xp_il(0, 1, 1, vector=True)
        xc_tr(i)
        xc_out(i)
        for b in range(RT):
            rgb_mm(i - 1, b)
            rgb_out(i - 1, b)
        x_stt(i + 1, 0)
        x_stt(i + 1, 1)
        xc_q(i)
        x_min(i + 1)
        x_max(i + 1)
        for b in range(RT):
            rgb_mm(i, b)
        i = MT - 1
        xc_tr(i)
        xp_il(1, 0, 0, vector=True)
        xp_il(1, 0, 1, vector=True)
        xp_q(1, 0)
        xp_q(0, 1)
        rgb_out(i - 1, 0)
        rgb_out(i - 1, 1)
        xc_out(i)
        rgb_out(i - 1, 2)
        for j in range(ST):
            coarse_mm(0, j)
        xp_il(1, 1, 0, vector=True)
        xc_q(i)
        xp_il(1, 1, 1, vector=True)
        xp_q(1, 1)
        coarse_put(0, 0, vector=False)
        coarse_put(0, 1, vector=False)
        coarse_put(0, 2, vector=False)
        coarse_put(0, 3, vector=True)
        for b in range(RT):
            rgb_mm(i, b)
            rgb_out(i, b, vector=(b == 1))
        for j in range(ST):
            coarse_mm(1, j)
            coarse_put(1, j, vector=(j % 2 == 0))
